import numpy as np
import ml_dtypes


def mxq(x, axis, fmt="e4m3"):
    dtype, down = {"e4m3": (ml_dtypes.float8_e4m3fn, 7), "e5m2": (ml_dtypes.float8_e5m2, 14)}[fmt]
    v = np.moveaxis(np.asarray(x, np.float32).astype(ml_dtypes.bfloat16).astype(np.float64), axis, -1)
    blocks = v.reshape(v.shape[:-1] + (-1, 32))
    amax = np.abs(blocks).max(-1, keepdims=True)
    byte = np.maximum(np.where(amax > 0, np.frexp(amax)[1] - 1 + 127, 0) - down, 1)
    scale = np.exp2(byte - 127.0)
    codes = (blocks / scale).astype(np.float32).astype(dtype).astype(np.float64)
    return np.moveaxis((codes * scale).reshape(v.shape), -1, axis)


WIDE = False


def mx_kscale(k):
    if not WIDE:
        return np.ones(k)
    levels = np.array([10, -10, 5, -5, 0])
    if k % 512:
        return np.exp2(np.random.permutation(np.resize(levels, k // 32))).repeat(32)
    a = np.empty((k // 512, 16))
    for p in range(k // 512):
        a[p, :8] = np.random.permutation(np.resize(levels, 8))
        for g in range(8):
            far = levels[np.abs(levels - a[p, g]) >= 10]
            a[p, g + 8] = far[np.random.randint(len(far))]
    return np.exp2(a.ravel()).repeat(32)


def f64(x):
    return np.asarray(x).astype(np.float64)


def striped(idx):
    return np.tile(idx.reshape(-1, 16).T, (8, 1)).astype(np.uint16)


def unstriped(offs):
    return offs[:16].T.reshape(-1).astype(np.int64)


E2M1 = np.array([0.0, 0.5, 1.0, 1.5, 2.0, 3.0, 4.0, 6.0, -0.0, -0.5, -1.0, -1.5, -2.0, -3.0, -4.0, -6.0])


def pack_weight(w, fmt):
    k, n = w.shape
    w = f64(np.asarray(w, np.float32).astype(ml_dtypes.bfloat16)).reshape(k // 32, 32, n)
    amax = np.abs(w).max(1)
    if fmt == "e4m3":
        byte = np.frexp(amax)[1] - 1 + 127 - 7
    else:
        mant, ex = np.frexp(amax / 6.0)
        byte = np.where(mant > 0.5, ex, ex - 1) + 127
    byte = np.clip(np.where(amax > 0, byte, 1), 1, 254)
    scaled = (w * np.exp2(127.0 - byte)[:, None, :]).reshape(k, n).astype(np.float32)
    by_word = np.ascontiguousarray(scaled.reshape(k // 512, 128, 4, n).transpose(0, 1, 3, 2))
    if fmt == "e4m3":
        words = by_word.astype(ml_dtypes.float8_e4m3fn).view(np.uint8)
    else:
        c = by_word.astype(ml_dtypes.float4_e2m1fn).view(np.uint8) & 0xF
        words = (c[..., 0::2] | (c[..., 1::2] << 4)).reshape(k // 512, 128, 2 * n)
    return np.ascontiguousarray(words), np.ascontiguousarray(byte.astype(np.uint8).reshape(k // 512, 16, n))


def unpack_weight(words, scales, fmt):
    g, _, n = scales.shape
    words = np.ascontiguousarray(words).reshape(g, 128, n, -1)
    if fmt == "e4m3":
        vals = words.view(ml_dtypes.float8_e4m3fn).astype(np.float64)
    else:
        nib = np.empty((g, 128, n, 4), np.uint8)
        nib[..., 0::2] = words & 0xF
        nib[..., 1::2] = words >> 4
        vals = E2M1[nib]
    vals = vals * np.repeat(np.exp2(scales.astype(np.float64) - 127.0), 8, axis=1)[..., None]
    return vals.transpose(0, 1, 3, 2).reshape(g * 512, n)


def gelu(v):
    return 0.5 * v * (1.0 + np.tanh(np.sqrt(2.0 / np.pi) * (v + 0.044715 * v**3)))


K, H, N, T, S, P, P2 = 1024, 1536, 512, 4096, 1024, 512, 256


def setup_inputs():
    n = np.random.standard_normal
    s = mx_kscale(K)[:, None]
    u = mx_kscale(H)[:, None]
    tab_words, tab_scales = pack_weight(n((K, T)) * s, "e4m3")
    w1 = n((K, H)) * 0.54 / np.sqrt(K) / s
    gain = np.exp(0.3 * n(H)) * u[:, 0]
    w4_words, w4_scales = pack_weight(n((H, N)) * 2.0 / np.sqrt(H) / u, "e2m1")
    return {
        "tab_words": tab_words,
        "tab_scales": tab_scales,
        "offs": striped(np.random.permutation(T)[:S]),
        "w1": w1.astype(np.float32),
        "gain": gain.astype(np.float32),
        "pos1": striped(np.random.permutation(S)[:P]),
        "pos2": striped(np.random.permutation(S)[:P]),
        "w4_words": w4_words,
        "w4_scales": w4_scales,
        "pos3": striped(np.random.permutation(P)[:P2]),
        "pos4": striped(np.random.permutation(P)[:P2]),
    }


def reference(tab_words, tab_scales, offs, w1, gain, pos1, pos2, w4_words, w4_scales, pos3, pos4):
    v = unpack_weight(tab_words, tab_scales, "e4m3")[:, unstriped(offs)]
    h = np.sin(mxq(f64(w1), 0, "e4m3").T @ v) * f64(gain)[:, None]
    z = np.minimum(h[:, unstriped(pos1)], h[:, unstriped(pos2)])
    w4 = unpack_weight(w4_words, w4_scales, "e2m1")
    y = w4.T @ mxq(z, 0, "e4m3")
    ya = y[:, unstriped(pos3)]
    yb = y[:, unstriped(pos4)]
    return np.abs(ya - yb) * ya

@@ -1,0 +1,227 @@
+import math
+from contextlib import ExitStack
+
+import concourse.mybir as mybir
+
+K, H, N, T, S, PAIRS, CUTS = 1024, 1536, 512, 4096, 1024, 512, 256
+FLOPS = 2 * K * H * S + 2 * H * N * PAIRS
+
+F32 = mybir.dt.float32
+BF16 = mybir.dt.bfloat16
+I32 = mybir.dt.int32
+U32 = mybir.dt.uint32
+U16 = mybir.dt.uint16
+U8 = mybir.dt.uint8
+FP8X4 = mybir.dt.float8_e4m3fn_x4
+FP4X4 = mybir.dt.float4_e2m1fn_x4
+ALU = mybir.AluOpType
+ACT = mybir.ActivationFunctionType
+
+P = 128
+PACK = 4
+PASS = P * PACK
+BANK = 512
+K_PASSES = K // PASS
+R_PASSES = H // PASS
+R_TILES = H // P
+N_TILES = N // P
+CAST_ROWS = 32
+TWO_PI = 2.0 * math.pi
+
+
+def tile_list_bucking_cut_contrast_kernel(
+    tc, tab_words, tab_scales, offs, w1, gain, pos1, pos2, w4_words, w4_scales, pos3, pos4, out
+):
+    nc = tc.nc
+    with ExitStack() as ctx:
+        keep = ctx.enter_context(tc.tile_pool(name="keep", bufs=1))
+        wraw_pool = ctx.enter_context(tc.tile_pool(name="wraw", bufs=4))
+        ring2 = ctx.enter_context(tc.tile_pool(name="ring2", bufs=2))
+        ring3 = ctx.enter_context(tc.tile_pool(name="ring3", bufs=3))
+        psum_x = ctx.enter_context(tc.psum_pool(name="psum_x", bufs=4))
+        psum_y = ctx.enter_context(tc.psum_pool(name="psum_y", bufs=1))
+
+        offs_sb = keep.tile([P, S // 16], U16, name="offs_sb")
+        pos1_sb = keep.tile([P, PAIRS // 16], U16, name="pos1_sb")
+        pos2_sb = keep.tile([P, PAIRS // 16], U16, name="pos2_sb")
+        pos3_sb = keep.tile([P, CUTS // 16], U16, name="pos3_sb")
+        pos4_sb = keep.tile([P, CUTS // 16], U16, name="pos4_sb")
+        v_sc = keep.tile([P, S], U8, name="v_sc", align_bytes=64)
+        v_w = [[keep.tile([P, BANK], U32, name=f"v_w{a}_{hf}", align_bytes=64) for hf in range(2)] for a in range(K_PASSES)]
+        gain_sb = keep.tile([P, R_PASSES, PACK], F32, name="gain_sb")
+        w4_w = keep.tile([P, R_PASSES, 2 * N], U8, name="w4_w", align_bytes=64)
+        w4_sc = keep.tile([P, R_PASSES, N], U8, name="w4_sc", align_bytes=64)
+        w1_w = [[keep.tile([P, PASS], U32, name=f"w1_w{b}_{a}", align_bytes=64) for a in range(K_PASSES)] for b in range(R_PASSES)]
+        w1_sc = [[keep.tile([P, PASS], U8, name=f"w1_sc{b}_{a}", align_bytes=64) for a in range(K_PASSES)] for b in range(R_PASSES)]
+        gain_rows = [keep.tile([P, PAIRS], F32, name=f"gain_rows{i}") for i in range(R_TILES)]
+        y_ps = [psum_y.tile([P, PAIRS], F32, name=f"y_ps{n}") for n in range(N_TILES)]
+
+        w_raw = {}
+
+        def load_w1(b, a):
+            raw = wraw_pool.tile([P, PACK, PASS], F32, name="raw")
+            rows = w1[a * PASS : (a + 1) * PASS, b * PASS : (b + 1) * PASS]
+            nc.sync.dma_start(out=raw[:], in_=rows.rearrange("(p j) c -> p j c", j=PACK))
+            w_raw[(b, a)] = raw
+
+        def quantise_w1(b, a):
+            raw = w_raw[(b, a)]
+            grouped = ring2.tile([P, PACK, P, PACK], BF16, name="grouped", align_bytes=64)
+            for m0 in range(0, P, CAST_ROWS):
+                nc.scalar.copy(
+                    out=grouped[:].rearrange("p t m j -> p m j t")[:, m0 : m0 + CAST_ROWS],
+                    in_=raw[:].rearrange("p j (m t) -> p m j t", t=PACK)[:, m0 : m0 + CAST_ROWS],
+                )
+            nc.vector.quantize_mx(
+                out=w1_w[b][a][:].bitcast(FP8X4),
+                scales=w1_sc[b][a][:],
+                in_=grouped[:].rearrange("p t m j -> p (t m j)"),
+            )
+
+        with tc.tile_pool(name="table", bufs=1) as table_pool:
+            tab_sc = table_pool.tile([P, T], U8, name="tab_sc", align_bytes=64)
+            tab_w = [table_pool.tile([P, T], U32, name=f"tab_w{a}", align_bytes=64) for a in range(K_PASSES)]
+
+            def load_table(a):
+                nc.sync.dma_start(out=tab_w[a][:].bitcast(I32), in_=tab_words[a].rearrange("p t i -> p (t i)").bitcast(I32))
+
+            nc.vector.memset(tab_sc[:].bitcast(I32), 0)
+            nc.vector.memset(w4_sc[:].rearrange("p a c -> p (a c)").bitcast(I32), 0)
+            nc.sync.dma_start(out=gain_sb[:], in_=gain.rearrange("(b p t) -> p b t", p=P, t=PACK))
+            nc.sync.dma_start(out=offs_sb[:], in_=offs)
+            for q in range(4):
+                nc.sync.dma_start(
+                    out=tab_sc[32 * q : 32 * q + 4 * K_PASSES, :].bitcast(I32),
+                    in_=tab_scales[:, 4 * q : 4 * q + 4, :].bitcast(I32),
+                )
+            load_w1(0, 0)
+            load_table(0)
+            load_w1(0, 1)
+            load_table(1)
+            nc.sync.dma_start(out=pos1_sb[:], in_=pos1)
+            nc.sync.dma_start(out=pos2_sb[:], in_=pos2)
+            load_w1(1, 0)
+            load_w1(1, 1)
+            nc.sync.dma_start(out=w4_w[:].bitcast(I32), in_=w4_words.rearrange("a p c -> p a c").bitcast(I32))
+            for q in range(4):
+                nc.sync.dma_start(
+                    out=w4_sc[32 * q : 32 * q + 4, :, :].bitcast(I32),
+                    in_=w4_scales[:, 4 * q : 4 * q + 4, :].rearrange("a q c -> q a c").bitcast(I32),
+                )
+            nc.sync.dma_start(out=pos3_sb[:], in_=pos3)
+            nc.sync.dma_start(out=pos4_sb[:], in_=pos4)
+
+            nc.vector.tensor_copy(out=v_sc[:], in_=tab_sc[:].indirect(offs_sb[:]))
+            half_cols = BANK // 16
+            for a in range(K_PASSES):
+                quantise_w1(0, a)
+                for hf in range(2):
+                    nc.vector.tensor_copy(
+                        out=v_w[a][hf][:], in_=tab_w[a][:].indirect(offs_sb[:, hf * half_cols : (hf + 1) * half_cols])
+                    )
+            load_w1(2, 0)
+            load_w1(2, 1)
+        late = ctx.enter_context(tc.tile_pool(name="late", bufs=3))
+        for i in range(R_TILES):
+            b, t = divmod(i, PACK)
+            nc.scalar.copy(out=gain_rows[i][:], in_=gain_sb[:, b, t : t + 1].to_broadcast([P, PAIRS]))
+
+        reduced = {}
+        picked = {}
+
+        def product_and_reduce(i):
+            b, t = divmod(i, PACK)
+            fold = ring3.tile([P, S], F32, name="fold")
+            turns = ring3.tile([P, S], U32, name="turns")
+            angle = ring3.tile([P, S], F32, name="angle")
+
+            def reduce(cols):
+                if b == 0:
+                    nc.vector.tensor_scalar(
+                        out=turns[:, cols].bitcast(I32), in0=fold[:, cols], scalar1=0.75, scalar2=None, op0=ALU.add
+                    )
+                else:
+                    nc.scalar.activation(out=turns[:, cols], in_=fold[:, cols], func=ACT.Copy, bias=0.75)
+                nc.vector.tensor_tensor(out=angle[:, cols], in0=fold[:, cols], in1=turns[:, cols].bitcast(I32), op=ALU.subtract)
+
+            for hf in range(2):
+                cols = slice(hf * BANK, (hf + 1) * BANK)
+                x_ps = psum_x.tile([P, BANK], F32, name="x_ps")
+                for a in range(K_PASSES):
+                    nc.tensor.matmul_mx(
+                        out=x_ps[:],
+                        lhsT=w1_w[b][a][:, t * P : (t + 1) * P].bitcast(FP8X4),
+                        lhsT_scale=w1_sc[b][a][:, t * P : (t + 1) * P],
+                        rhs=v_w[a][hf][:].bitcast(FP8X4),
+                        rhs_scale=v_sc[4 * a : P, cols],
+                        start=(a == 0),
+                        stop=(a == K_PASSES - 1),
+                    )
+                nc.scalar.activation(out=fold[:, cols], in_=x_ps[:], func=ACT.Abs, scale=1.0 / TWO_PI, bias=-0.25)
+                if i == 0:
+                    reduce(cols)
+            if i > 0:
+                reduce(slice(0, S))
+            reduced[i] = angle
+
+        def features_and_pick(i):
+            b, t = divmod(i, PACK)
+            sine = ring3.tile([P, S], F32, name="sine")
+            nc.scalar.activation(out=sine[:], in_=reduced[i][:], func=ACT.Sin, scale=-TWO_PI, bias=-1.5 * math.pi)
+            if t == 0:
+                picked[b] = (
+                    ring2.tile([P, PACK, PAIRS], F32, name="butt"),
+                    ring2.tile([P, PACK, PAIRS], F32, name="top"),
+                )
+            butt, top = picked[b]
+            nc.vector.tensor_tensor(out=butt[:, t, :], in0=sine[:].indirect(pos1_sb[:]), in1=gain_rows[i][:], op=ALU.mult)
+            nc.vector.tensor_tensor(out=top[:, t, :], in0=sine[:].indirect(pos2_sb[:]), in1=gain_rows[i][:], op=ALU.mult)
+
+        def second_product(b):
+            butt, top = picked[b]
+            z = ring2.tile([P, PAIRS, PACK], BF16, name="z", align_bytes=64)
+            z_w = ring2.tile([P, PAIRS], U32, name="z_w", align_bytes=64)
+            z_sc = ring2.tile([P, PAIRS], U8, name="z_sc", align_bytes=64)
+            nc.vector.tensor_tensor(
+                out=z[:].rearrange("p (c i) t -> p c t i", i=4),
+                in0=butt[:].rearrange("p t (c i) -> p c t i", i=4),
+                in1=top[:].rearrange("p t (c i) -> p c t i", i=4),
+                op=ALU.min,
+            )
+            nc.vector.quantize_mx(out=z_w[:].bitcast(FP8X4), scales=z_sc[:], in_=z[:].rearrange("p m t -> p (m t)"))
+            for n in range(N_TILES):
+                nc.tensor.matmul_mx(
+                    out=y_ps[n][:],
+                    lhsT=w4_w[:, b, 2 * n * P : 2 * (n + 1) * P].bitcast(FP4X4),
+                    lhsT_scale=w4_sc[:, b, n * P : (n + 1) * P],
+                    rhs=z_w[:].bitcast(FP8X4),
+                    rhs_scale=z_sc[:],
+                    start=(b == 0),
+                    stop=(b == R_PASSES - 1),
+                )
+
+        started = 0
+        for i in range(R_TILES):
+            b, t = divmod(i, PACK)
+            ahead = 1 if i < 2 else 2
+            while started <= min(R_TILES - 1, i + ahead):
+                product_and_reduce(started)
+                started = started + 1
+            features_and_pick(i)
+            if t < K_PASSES and b + 1 < R_PASSES:
+                quantise_w1(b + 1, t)
+            if t == PACK - 1:
+                second_product(b)
+
+        for n in range(N_TILES):
+            y = late.tile([P, PAIRS], F32, name="y")
+            first = late.tile([P, CUTS], F32, name="first")
+            diff = late.tile([P, CUTS], F32, name="diff")
+            dist = late.tile([P, CUTS], F32, name="dist")
+            res = late.tile([P, CUTS], F32, name="res")
+            nc.scalar.copy(out=y[:], in_=y_ps[n][:])
+            nc.vector.tensor_copy(out=first[:], in_=y[:].indirect(pos3_sb[:]))
+            nc.vector.tensor_tensor(out=diff[:], in0=y[:].indirect(pos4_sb[:]), in1=first[:], op=ALU.subtract)
+            nc.scalar.activation(out=dist[:], in_=diff[:], func=ACT.Abs)
+            nc.vector.tensor_tensor(out=res[:], in0=dist[:], in1=first[:], op=ALU.mult)
+            nc.sync.dma_start(out=out[n * P : (n + 1) * P, :], in_=res[:])

@@ -26,6 +26,9 @@ R_PASSES = H // PASS
 R_TILES = H // P
 N_TILES = N // P
 CAST_ROWS = 32
+HALF = PAIRS // 2
+X_BANKS = 3
+VECTOR_COUNTS = 3
 TWO_PI = 2.0 * math.pi
 
 
@@ -38,7 +41,7 @@ def tile_list_bucking_cut_contrast_kernel(
         wraw_pool = ctx.enter_context(tc.tile_pool(name="wraw", bufs=4))
         ring2 = ctx.enter_context(tc.tile_pool(name="ring2", bufs=2))
         ring3 = ctx.enter_context(tc.tile_pool(name="ring3", bufs=3))
-        psum_x = ctx.enter_context(tc.psum_pool(name="psum_x", bufs=4))
+        psum_x = ctx.enter_context(tc.psum_pool(name="psum_x", bufs=X_BANKS))
         psum_y = ctx.enter_context(tc.psum_pool(name="psum_y", bufs=1))
 
         offs_sb = keep.tile([P, S // 16], U16, name="offs_sb")
@@ -54,7 +57,17 @@ def tile_list_bucking_cut_contrast_kernel(
         w1_w = [[keep.tile([P, PASS], U32, name=f"w1_w{b}_{a}", align_bytes=64) for a in range(K_PASSES)] for b in range(R_PASSES)]
         w1_sc = [[keep.tile([P, PASS], U8, name=f"w1_sc{b}_{a}", align_bytes=64) for a in range(K_PASSES)] for b in range(R_PASSES)]
         gain_rows = [keep.tile([P, PAIRS], F32, name=f"gain_rows{i}") for i in range(R_TILES)]
-        y_ps = [psum_y.tile([P, PAIRS], F32, name=f"y_ps{n}") for n in range(N_TILES)]
+        y_groups = [[(0, 1), (2, 3)], [(0,), (1,), (2, 3)]]
+        y_ps = {}
+        for hf in range(2):
+            for group in y_groups[hf]:
+                bank = psum_y.tile([P, len(group), HALF], F32, name=f"y_ps{hf}_{group[0]}")
+                for place, n in enumerate(group):
+                    y_ps[(hf, n)] = (bank[:, place, :], n == group[0], n == group[-1])
+
+        warm = keep.tile([P, 16], F32, name="warm")
+        nc.gpsimd.memset(warm[:, 0:1], 0.0)
+        nc.scalar.activation(out=warm[:, 8:9], in_=warm[:, 0:1], func=ACT.Sin, scale=-TWO_PI, bias=0.5 * math.pi)
 
         w_raw = {}
 
@@ -121,86 +134,144 @@ def tile_list_bucking_cut_contrast_kernel(
                     )
             load_w1(2, 0)
             load_w1(2, 1)
-        late = ctx.enter_context(tc.tile_pool(name="late", bufs=3))
+        late = ctx.enter_context(tc.tile_pool(name="late", bufs=1))
         for i in range(R_TILES):
             b, t = divmod(i, PACK)
             nc.scalar.copy(out=gain_rows[i][:], in_=gain_sb[:, b, t : t + 1].to_broadcast([P, PAIRS]))
 
         reduced = {}
         picked = {}
+        sines = {}
 
-        def product_and_reduce(i):
+        halves = (slice(0, BANK), slice(BANK, S))
+
+        def first_pass(i, hf, a, x_ps):
             b, t = divmod(i, PACK)
+            nc.tensor.matmul_mx(
+                out=x_ps[:],
+                lhsT=w1_w[b][a][:, t * P : (t + 1) * P].bitcast(FP8X4),
+                lhsT_scale=w1_sc[b][a][:, t * P : (t + 1) * P],
+                rhs=v_w[a][hf][:].bitcast(FP8X4),
+                rhs_scale=v_sc[4 * a : P, halves[hf]],
+                start=(a == 0),
+                stop=(a == K_PASSES - 1),
+            )
+
+        def new_tiles(i):
             fold = ring3.tile([P, S], F32, name="fold")
             turns = ring3.tile([P, S], U32, name="turns")
             angle = ring3.tile([P, S], F32, name="angle")
+            reduced[i] = angle
+            return fold, turns, angle
 
-            def reduce(cols):
-                if b == 0:
-                    nc.vector.tensor_scalar(
-                        out=turns[:, cols].bitcast(I32), in0=fold[:, cols], scalar1=0.75, scalar2=None, op0=ALU.add
-                    )
-                else:
-                    nc.scalar.activation(out=turns[:, cols], in_=fold[:, cols], func=ACT.Copy, bias=0.75)
-                nc.vector.tensor_tensor(out=angle[:, cols], in0=fold[:, cols], in1=turns[:, cols].bitcast(I32), op=ALU.subtract)
+        def fold_out(tiles, hf, x_ps):
+            nc.scalar.activation(out=tiles[0][:, halves[hf]], in_=x_ps[:], func=ACT.Abs, scale=1.0 / TWO_PI, bias=-0.25)
 
+        def reduce(i, tiles, cols):
+            fold, turns, angle = tiles
+            if i < VECTOR_COUNTS:
+                nc.vector.tensor_scalar(
+                    out=turns[:, cols].bitcast(I32), in0=fold[:, cols], scalar1=-0.25, scalar2=None, op0=ALU.add
+                )
+            else:
+                nc.scalar.activation(out=turns[:, cols], in_=fold[:, cols], func=ACT.Copy, bias=-0.25)
+            nc.vector.tensor_tensor(out=angle[:, cols], in0=fold[:, cols], in1=turns[:, cols].bitcast(I32), op=ALU.subtract)
+
+        def take_sine(i, cols):
+            if i not in sines:
+                sines[i] = ring3.tile([P, S], F32, name="sine")
+            nc.scalar.activation(out=sines[i][:, cols], in_=reduced[i][:, cols], func=ACT.Sin, scale=-TWO_PI, bias=0.5 * math.pi)
+
+        def product_and_reduce(i):
+            tiles = new_tiles(i)
             for hf in range(2):
-                cols = slice(hf * BANK, (hf + 1) * BANK)
                 x_ps = psum_x.tile([P, BANK], F32, name="x_ps")
                 for a in range(K_PASSES):
-                    nc.tensor.matmul_mx(
-                        out=x_ps[:],
-                        lhsT=w1_w[b][a][:, t * P : (t + 1) * P].bitcast(FP8X4),
-                        lhsT_scale=w1_sc[b][a][:, t * P : (t + 1) * P],
-                        rhs=v_w[a][hf][:].bitcast(FP8X4),
-                        rhs_scale=v_sc[4 * a : P, cols],
-                        start=(a == 0),
-                        stop=(a == K_PASSES - 1),
-                    )
-                nc.scalar.activation(out=fold[:, cols], in_=x_ps[:], func=ACT.Abs, scale=1.0 / TWO_PI, bias=-0.25)
-                if i == 0:
-                    reduce(cols)
-            if i > 0:
-                reduce(slice(0, S))
-            reduced[i] = angle
+                    first_pass(i, hf, a, x_ps)
+                fold_out(tiles, hf, x_ps)
+            reduce(i, tiles, slice(0, S))
+
+        def start_up():
+            tiles = [new_tiles(i) for i in range(2)]
+            units = [(i, hf) for hf in range(2) for i in range(2)]
+            banks = {}
+            for unit in units[:X_BANKS]:
+                banks[unit] = psum_x.tile([P, BANK], F32, name="x_ps")
+                first_pass(unit[0], unit[1], 0, banks[unit])
+            for unit in units:
+                if unit not in banks:
+                    banks[unit] = psum_x.tile([P, BANK], F32, name="x_ps")
+                    first_pass(unit[0], unit[1], 0, banks[unit])
+                first_pass(unit[0], unit[1], 1, banks[unit])
+                fold_out(tiles[unit[0]], unit[1], banks[unit])
+            for i in range(2):
+                for hf in range(2):
+                    reduce(i, tiles[i], halves[hf])
+                    if i == 0:
+                        take_sine(0, halves[hf])
+
+        def pick(i, into, pos, cols):
+            t = i % PACK
+            nc.vector.tensor_tensor(
+                out=into[:, t, cols],
+                in0=sines[i][:].indirect(pos[:, cols.start // 16 : cols.stop // 16]),
+                in1=gain_rows[i][:, cols],
+                op=ALU.mult,
+            )
 
         def features_and_pick(i):
             b, t = divmod(i, PACK)
-            sine = ring3.tile([P, S], F32, name="sine")
-            nc.scalar.activation(out=sine[:], in_=reduced[i][:], func=ACT.Sin, scale=-TWO_PI, bias=-1.5 * math.pi)
+            if i > 0:
+                take_sine(i, slice(0, S))
             if t == 0:
                 picked[b] = (
                     ring2.tile([P, PACK, PAIRS], F32, name="butt"),
                     ring2.tile([P, PACK, PAIRS], F32, name="top"),
                 )
-            butt, top = picked[b]
-            nc.vector.tensor_tensor(out=butt[:, t, :], in0=sine[:].indirect(pos1_sb[:]), in1=gain_rows[i][:], op=ALU.mult)
-            nc.vector.tensor_tensor(out=top[:, t, :], in0=sine[:].indirect(pos2_sb[:]), in1=gain_rows[i][:], op=ALU.mult)
+            if t < PACK - 1:
+                pick(i, picked[b][0], pos1_sb, slice(0, PAIRS))
+                pick(i, picked[b][1], pos2_sb, slice(0, PAIRS))
 
         def second_product(b):
             butt, top = picked[b]
-            z = ring2.tile([P, PAIRS, PACK], BF16, name="z", align_bytes=64)
-            z_w = ring2.tile([P, PAIRS], U32, name="z_w", align_bytes=64)
-            z_sc = ring2.tile([P, PAIRS], U8, name="z_sc", align_bytes=64)
-            nc.vector.tensor_tensor(
-                out=z[:].rearrange("p (c i) t -> p c t i", i=4),
-                in0=butt[:].rearrange("p t (c i) -> p c t i", i=4),
-                in1=top[:].rearrange("p t (c i) -> p c t i", i=4),
-                op=ALU.min,
-            )
-            nc.vector.quantize_mx(out=z_w[:].bitcast(FP8X4), scales=z_sc[:], in_=z[:].rearrange("p m t -> p (m t)"))
-            for n in range(N_TILES):
-                nc.tensor.matmul_mx(
-                    out=y_ps[n][:],
-                    lhsT=w4_w[:, b, 2 * n * P : 2 * (n + 1) * P].bitcast(FP4X4),
-                    lhsT_scale=w4_sc[:, b, n * P : (n + 1) * P],
-                    rhs=z_w[:].bitcast(FP8X4),
-                    rhs_scale=z_sc[:],
-                    start=(b == 0),
-                    stop=(b == R_PASSES - 1),
+            last = b * PACK + PACK - 1
+            pairs = (slice(0, HALF), slice(HALF, PAIRS))
+            z = [ring2.tile([P, HALF, PACK], BF16, name=f"z{hf}", align_bytes=64) for hf in range(2)]
+
+            def smaller(hf):
+                nc.vector.tensor_tensor(
+                    out=z[hf][:].rearrange("p (c i) t -> p c t i", i=2),
+                    in0=butt[:, :, pairs[hf]].rearrange("p t (c i) -> p c t i", i=2),
+                    in1=top[:, :, pairs[hf]].rearrange("p t (c i) -> p c t i", i=2),
+                    op=ALU.min,
                 )
 
-        started = 0
+            def multiply(hf):
+                z_w = ring2.tile([P, HALF], U32, name=f"z_w{hf}", align_bytes=64)
+                z_sc = ring2.tile([P, HALF], U8, name=f"z_sc{hf}", align_bytes=64)
+                nc.vector.quantize_mx(out=z_w[:].bitcast(FP8X4), scales=z_sc[:], in_=z[hf][:].rearrange("p m t -> p (m t)"))
+                for n in range(N_TILES):
+                    nc.tensor.matmul_mx(
+                        out=y_ps[(hf, n)][0],
+                        lhsT=w4_w[:, b, 2 * n * P : 2 * (n + 1) * P].bitcast(FP4X4),
+                        lhsT_scale=w4_sc[:, b, n * P : (n + 1) * P],
+                        rhs=z_w[:].bitcast(FP8X4),
+                        rhs_scale=z_sc[:],
+                        start=(b == 0 and y_ps[(hf, n)][1]),
+                        stop=(b == R_PASSES - 1 and y_ps[(hf, n)][2]),
+                    )
+
+            pick(last, butt, pos1_sb, pairs[0])
+            pick(last, top, pos2_sb, pairs[0])
+            pick(last, butt, pos1_sb, pairs[1])
+            smaller(0)
+            pick(last, top, pos2_sb, pairs[1])
+            multiply(0)
+            smaller(1)
+            multiply(1)
+
+        start_up()
+        started = 2
         for i in range(R_TILES):
             b, t = divmod(i, PACK)
             ahead = 1 if i < 2 else 2
@@ -213,15 +284,29 @@ def tile_list_bucking_cut_contrast_kernel(
             if t == PACK - 1:
                 second_product(b)
 
-        for n in range(N_TILES):
-            y = late.tile([P, PAIRS], F32, name="y")
-            first = late.tile([P, CUTS], F32, name="first")
-            diff = late.tile([P, CUTS], F32, name="diff")
-            dist = late.tile([P, CUTS], F32, name="dist")
-            res = late.tile([P, CUTS], F32, name="res")
-            nc.scalar.copy(out=y[:], in_=y_ps[n][:])
-            nc.vector.tensor_copy(out=first[:], in_=y[:].indirect(pos3_sb[:]))
-            nc.vector.tensor_tensor(out=diff[:], in0=y[:].indirect(pos4_sb[:]), in1=first[:], op=ALU.subtract)
-            nc.scalar.activation(out=dist[:], in_=diff[:], func=ACT.Abs)
-            nc.vector.tensor_tensor(out=res[:], in0=dist[:], in1=first[:], op=ALU.mult)
-            nc.sync.dma_start(out=out[n * P : (n + 1) * P, :], in_=res[:])
+        y = [late.tile([P, PAIRS], F32, name=f"y{n}") for n in range(N_TILES)]
+        first = [late.tile([P, CUTS], F32, name=f"first{n}") for n in range(N_TILES)]
+        diff = [late.tile([P, CUTS], F32, name=f"diff{n}") for n in range(N_TILES)]
+        dist = [late.tile([P, CUTS], F32, name=f"dist{n}") for n in range(N_TILES)]
+        res = [late.tile([P, CUTS], F32, name=f"res{n}") for n in range(N_TILES)]
+        order = (0, 1, 2, 3)
+        for hf in range(2):
+            for n in order:
+                source = y_ps[(hf, n)][0]
+                if hf == 1 and n == 1:
+                    nc.vector.tensor_copy(out=y[n][:, hf * HALF : (hf + 1) * HALF], in_=source)
+                else:
+                    nc.scalar.copy(out=y[n][:, hf * HALF : (hf + 1) * HALF], in_=source)
+
+        def finish(n):
+            nc.vector.tensor_tensor(out=res[n][:], in0=dist[n][:], in1=first[n][:], op=ALU.mult)
+            nc.sync.dma_start(out=out[n * P : (n + 1) * P, :], in_=res[n][:])
+
+        for pair in (order[:2], order[2:]):
+            for n in pair:
+                nc.vector.tensor_copy(out=first[n][:], in_=y[n][:].indirect(pos3_sb[:]))
+            for n in pair:
+                nc.vector.tensor_tensor(out=diff[n][:], in0=y[n][:].indirect(pos4_sb[:]), in1=first[n][:], op=ALU.subtract)
+                nc.scalar.activation(out=dist[n][:], in_=diff[n][:], func=ACT.Abs)
+        for n in order:
+            finish(n)

@@ -49,6 +49,7 @@ def tile_list_bucking_cut_contrast_kernel(
         pos2_sb = keep.tile([P, PAIRS // 16], U16, name="pos2_sb")
         pos3_sb = keep.tile([P, CUTS // 16], U16, name="pos3_sb")
         pos4_sb = keep.tile([P, CUTS // 16], U16, name="pos4_sb")
+        v_rows = keep.tile([P, S], U8, name="v_rows", align_bytes=64)
         v_sc = keep.tile([P, S], U8, name="v_sc", align_bytes=64)
         v_w = [[keep.tile([P, BANK], U32, name=f"v_w{a}_{hf}", align_bytes=64) for hf in range(2)] for a in range(K_PASSES)]
         gain_sb = keep.tile([P, R_PASSES, PACK], F32, name="gain_sb")
@@ -98,15 +99,12 @@ def tile_list_bucking_cut_contrast_kernel(
             def load_table(a):
                 nc.sync.dma_start(out=tab_w[a][:].bitcast(I32), in_=tab_words[a].rearrange("p t i -> p (t i)").bitcast(I32))
 
-            nc.vector.memset(tab_sc[:].bitcast(I32), 0)
+            nc.gpsimd.memset(tab_sc[32:64, :].bitcast(I32), 0)
+            nc.vector.memset(tab_sc[64:P, :].bitcast(I32), 0)
             nc.vector.memset(w4_sc[:].rearrange("p a c -> p (a c)").bitcast(I32), 0)
-            nc.sync.dma_start(out=gain_sb[:], in_=gain.rearrange("(b p t) -> p b t", p=P, t=PACK))
             nc.sync.dma_start(out=offs_sb[:], in_=offs)
-            for q in range(4):
-                nc.sync.dma_start(
-                    out=tab_sc[32 * q : 32 * q + 4 * K_PASSES, :].bitcast(I32),
-                    in_=tab_scales[:, 4 * q : 4 * q + 4, :].bitcast(I32),
-                )
+            nc.sync.dma_start(out=tab_sc[0:32, :].bitcast(I32), in_=tab_scales.rearrange("a q t -> (a q) t").bitcast(I32))
+            nc.sync.dma_start(out=gain_sb[:], in_=gain.rearrange("(b p t) -> p b t", p=P, t=PACK))
             load_w1(0, 0)
             load_table(0)
             load_w1(0, 1)
@@ -124,7 +122,15 @@ def tile_list_bucking_cut_contrast_kernel(
             nc.sync.dma_start(out=pos3_sb[:], in_=pos3)
             nc.sync.dma_start(out=pos4_sb[:], in_=pos4)
 
-            nc.vector.tensor_copy(out=v_sc[:], in_=tab_sc[:].indirect(offs_sb[:]))
+            nc.vector.tensor_copy(out=v_rows[:], in_=tab_sc[:].indirect(offs_sb[:]))
+            nc.vector.tensor_copy(out=v_sc[:].bitcast(I32), in_=v_rows[:].bitcast(I32))
+            for a in range(K_PASSES):
+                for q in range(4):
+                    if (a, q) != (0, 0):
+                        nc.gpsimd.dma_start(
+                            out=v_sc[32 * q + 4 * a : 32 * q + 4 * a + 4, :].bitcast(I32),
+                            in_=v_rows[16 * a + 4 * q : 16 * a + 4 * q + 4, :].bitcast(I32),
+                        )
             half_cols = BANK // 16
             for a in range(K_PASSES):
                 quantise_w1(0, a)

import math
from contextlib import ExitStack

import concourse.mybir as mybir

K, H, N, T, S, PAIRS, CUTS = 1024, 1536, 512, 4096, 1024, 512, 256
FLOPS = 2 * K * H * S + 2 * H * N * PAIRS

F32 = mybir.dt.float32
BF16 = mybir.dt.bfloat16
I32 = mybir.dt.int32
U32 = mybir.dt.uint32
U16 = mybir.dt.uint16
U8 = mybir.dt.uint8
FP8X4 = mybir.dt.float8_e4m3fn_x4
FP4X4 = mybir.dt.float4_e2m1fn_x4
ALU = mybir.AluOpType
ACT = mybir.ActivationFunctionType

P = 128
PACK = 4
PASS = P * PACK
BANK = 512
K_PASSES = K // PASS
R_PASSES = H // PASS
R_TILES = H // P
N_TILES = N // P
CAST_ROWS = 32
HALF = PAIRS // 2
X_BANKS = 3
VECTOR_COUNTS = 3
TWO_PI = 2.0 * math.pi


def tile_list_bucking_cut_contrast_kernel(
    tc, tab_words, tab_scales, offs, w1, gain, pos1, pos2, w4_words, w4_scales, pos3, pos4, out
):
    nc = tc.nc
    with ExitStack() as ctx:
        keep = ctx.enter_context(tc.tile_pool(name="keep", bufs=1))
        wraw_pool = ctx.enter_context(tc.tile_pool(name="wraw", bufs=4))
        ring2 = ctx.enter_context(tc.tile_pool(name="ring2", bufs=2))
        ring3 = ctx.enter_context(tc.tile_pool(name="ring3", bufs=3))
        psum_x = ctx.enter_context(tc.psum_pool(name="psum_x", bufs=X_BANKS))
        psum_y = ctx.enter_context(tc.psum_pool(name="psum_y", bufs=1))

        offs_sb = keep.tile([P, S // 16], U16, name="offs_sb")
        pos1_sb = keep.tile([P, PAIRS // 16], U16, name="pos1_sb")
        pos2_sb = keep.tile([P, PAIRS // 16], U16, name="pos2_sb")
        pos3_sb = keep.tile([P, CUTS // 16], U16, name="pos3_sb")
        pos4_sb = keep.tile([P, CUTS // 16], U16, name="pos4_sb")
        v_rows = keep.tile([P, S], U8, name="v_rows", align_bytes=64)
        v_sc = keep.tile([P, S], U8, name="v_sc", align_bytes=64)
        v_w = [[keep.tile([P, BANK], U32, name=f"v_w{a}_{hf}", align_bytes=64) for hf in range(2)] for a in range(K_PASSES)]
        gain_sb = keep.tile([P, R_PASSES, PACK], F32, name="gain_sb")
        w4_w = keep.tile([P, R_PASSES, 2 * N], U8, name="w4_w", align_bytes=64)
        w4_sc = keep.tile([P, R_PASSES, N], U8, name="w4_sc", align_bytes=64)
        w1_w = [[keep.tile([P, PASS], U32, name=f"w1_w{b}_{a}", align_bytes=64) for a in range(K_PASSES)] for b in range(R_PASSES)]
        w1_sc = [[keep.tile([P, PASS], U8, name=f"w1_sc{b}_{a}", align_bytes=64) for a in range(K_PASSES)] for b in range(R_PASSES)]
        gain_rows = [keep.tile([P, PAIRS], F32, name=f"gain_rows{i}") for i in range(R_TILES)]
        y_groups = [[(0, 1), (2, 3)], [(0,), (1,), (2, 3)]]
        y_ps = {}
        for hf in range(2):
            for group in y_groups[hf]:
                bank = psum_y.tile([P, len(group), HALF], F32, name=f"y_ps{hf}_{group[0]}")
                for place, n in enumerate(group):
                    y_ps[(hf, n)] = (bank[:, place, :], n == group[0], n == group[-1])

        warm = keep.tile([P, 16], F32, name="warm")
        nc.gpsimd.memset(warm[:, 0:1], 0.0)
        nc.scalar.activation(out=warm[:, 8:9], in_=warm[:, 0:1], func=ACT.Sin, scale=-TWO_PI, bias=0.5 * math.pi)

        w_raw = {}

        def load_w1(b, a):
            raw = wraw_pool.tile([P, PACK, PASS], F32, name="raw")
            rows = w1[a * PASS : (a + 1) * PASS, b * PASS : (b + 1) * PASS]
            nc.sync.dma_start(out=raw[:], in_=rows.rearrange("(p j) c -> p j c", j=PACK))
            w_raw[(b, a)] = raw

        def quantise_w1(b, a):
            raw = w_raw[(b, a)]
            grouped = ring2.tile([P, PACK, P, PACK], BF16, name="grouped", align_bytes=64)
            for m0 in range(0, P, CAST_ROWS):
                nc.scalar.copy(
                    out=grouped[:].rearrange("p t m j -> p m j t")[:, m0 : m0 + CAST_ROWS],
                    in_=raw[:].rearrange("p j (m t) -> p m j t", t=PACK)[:, m0 : m0 + CAST_ROWS],
                )
            nc.vector.quantize_mx(
                out=w1_w[b][a][:].bitcast(FP8X4),
                scales=w1_sc[b][a][:],
                in_=grouped[:].rearrange("p t m j -> p (t m j)"),
            )

        with tc.tile_pool(name="table", bufs=1) as table_pool:
            tab_sc = table_pool.tile([P, T], U8, name="tab_sc", align_bytes=64)
            tab_w = [table_pool.tile([P, T], U32, name=f"tab_w{a}", align_bytes=64) for a in range(K_PASSES)]

            def load_table(a):
                nc.sync.dma_start(out=tab_w[a][:].bitcast(I32), in_=tab_words[a].rearrange("p t i -> p (t i)").bitcast(I32))

            nc.gpsimd.memset(tab_sc[32:64, :].bitcast(I32), 0)
            nc.vector.memset(tab_sc[64:P, :].bitcast(I32), 0)
            nc.vector.memset(w4_sc[:].rearrange("p a c -> p (a c)").bitcast(I32), 0)
            nc.sync.dma_start(out=offs_sb[:], in_=offs)
            nc.sync.dma_start(out=tab_sc[0:32, :].bitcast(I32), in_=tab_scales.rearrange("a q t -> (a q) t").bitcast(I32))
            nc.sync.dma_start(out=gain_sb[:], in_=gain.rearrange("(b p t) -> p b t", p=P, t=PACK))
            load_w1(0, 0)
            load_table(0)
            load_w1(0, 1)
            load_table(1)
            nc.sync.dma_start(out=pos1_sb[:], in_=pos1)
            nc.sync.dma_start(out=pos2_sb[:], in_=pos2)
            load_w1(1, 0)
            load_w1(1, 1)
            nc.sync.dma_start(out=w4_w[:].bitcast(I32), in_=w4_words.rearrange("a p c -> p a c").bitcast(I32))
            for q in range(4):
                nc.sync.dma_start(
                    out=w4_sc[32 * q : 32 * q + 4, :, :].bitcast(I32),
                    in_=w4_scales[:, 4 * q : 4 * q + 4, :].rearrange("a q c -> q a c").bitcast(I32),
                )
            nc.sync.dma_start(out=pos3_sb[:], in_=pos3)
            nc.sync.dma_start(out=pos4_sb[:], in_=pos4)

            nc.vector.tensor_copy(out=v_rows[:], in_=tab_sc[:].indirect(offs_sb[:]))
            nc.vector.tensor_copy(out=v_sc[:].bitcast(I32), in_=v_rows[:].bitcast(I32))
            for a in range(K_PASSES):
                for q in range(4):
                    if (a, q) != (0, 0):
                        nc.gpsimd.dma_start(
                            out=v_sc[32 * q + 4 * a : 32 * q + 4 * a + 4, :].bitcast(I32),
                            in_=v_rows[16 * a + 4 * q : 16 * a + 4 * q + 4, :].bitcast(I32),
                        )
            half_cols = BANK // 16
            for a in range(K_PASSES):
                quantise_w1(0, a)
                for hf in range(2):
                    nc.vector.tensor_copy(
                        out=v_w[a][hf][:], in_=tab_w[a][:].indirect(offs_sb[:, hf * half_cols : (hf + 1) * half_cols])
                    )
            load_w1(2, 0)
            load_w1(2, 1)
        late = ctx.enter_context(tc.tile_pool(name="late", bufs=1))
        for i in range(R_TILES):
            b, t = divmod(i, PACK)
            nc.scalar.copy(out=gain_rows[i][:], in_=gain_sb[:, b, t : t + 1].to_broadcast([P, PAIRS]))

        reduced = {}
        picked = {}
        sines = {}

        halves = (slice(0, BANK), slice(BANK, S))

        def first_pass(i, hf, a, x_ps):
            b, t = divmod(i, PACK)
            nc.tensor.matmul_mx(
                out=x_ps[:],
                lhsT=w1_w[b][a][:, t * P : (t + 1) * P].bitcast(FP8X4),
                lhsT_scale=w1_sc[b][a][:, t * P : (t + 1) * P],
                rhs=v_w[a][hf][:].bitcast(FP8X4),
                rhs_scale=v_sc[4 * a : P, halves[hf]],
                start=(a == 0),
                stop=(a == K_PASSES - 1),
            )

        def new_tiles(i):
            fold = ring3.tile([P, S], F32, name="fold")
            turns = ring3.tile([P, S], U32, name="turns")
            angle = ring3.tile([P, S], F32, name="angle")
            reduced[i] = angle
            return fold, turns, angle

        def fold_out(tiles, hf, x_ps):
            nc.scalar.activation(out=tiles[0][:, halves[hf]], in_=x_ps[:], func=ACT.Abs, scale=1.0 / TWO_PI, bias=-0.25)

        def reduce(i, tiles, cols):
            fold, turns, angle = tiles
            if i < VECTOR_COUNTS:
                nc.vector.tensor_scalar(
                    out=turns[:, cols].bitcast(I32), in0=fold[:, cols], scalar1=-0.25, scalar2=None, op0=ALU.add
                )
            else:
                nc.scalar.activation(out=turns[:, cols], in_=fold[:, cols], func=ACT.Copy, bias=-0.25)
            nc.vector.tensor_tensor(out=angle[:, cols], in0=fold[:, cols], in1=turns[:, cols].bitcast(I32), op=ALU.subtract)

        def take_sine(i, cols):
            if i not in sines:
                sines[i] = ring3.tile([P, S], F32, name="sine")
            nc.scalar.activation(out=sines[i][:, cols], in_=reduced[i][:, cols], func=ACT.Sin, scale=-TWO_PI, bias=0.5 * math.pi)

        def product_and_reduce(i):
            tiles = new_tiles(i)
            for hf in range(2):
                x_ps = psum_x.tile([P, BANK], F32, name="x_ps")
                for a in range(K_PASSES):
                    first_pass(i, hf, a, x_ps)
                fold_out(tiles, hf, x_ps)
            reduce(i, tiles, slice(0, S))

        def start_up():
            tiles = [new_tiles(i) for i in range(2)]
            units = [(i, hf) for hf in range(2) for i in range(2)]
            banks = {}
            for unit in units[:X_BANKS]:
                banks[unit] = psum_x.tile([P, BANK], F32, name="x_ps")
                first_pass(unit[0], unit[1], 0, banks[unit])
            for unit in units:
                if unit not in banks:
                    banks[unit] = psum_x.tile([P, BANK], F32, name="x_ps")
                    first_pass(unit[0], unit[1], 0, banks[unit])
                first_pass(unit[0], unit[1], 1, banks[unit])
                fold_out(tiles[unit[0]], unit[1], banks[unit])
            for i in range(2):
                for hf in range(2):
                    reduce(i, tiles[i], halves[hf])
                    if i == 0:
                        take_sine(0, halves[hf])

        def pick(i, into, pos, cols):
            t = i % PACK
            nc.vector.tensor_tensor(
                out=into[:, t, cols],
                in0=sines[i][:].indirect(pos[:, cols.start // 16 : cols.stop // 16]),
                in1=gain_rows[i][:, cols],
                op=ALU.mult,
            )

        def features_and_pick(i):
            b, t = divmod(i, PACK)
            if i > 0:
                take_sine(i, slice(0, S))
            if t == 0:
                picked[b] = (
                    ring2.tile([P, PACK, PAIRS], F32, name="butt"),
                    ring2.tile([P, PACK, PAIRS], F32, name="top"),
                )
            if t < PACK - 1:
                pick(i, picked[b][0], pos1_sb, slice(0, PAIRS))
                pick(i, picked[b][1], pos2_sb, slice(0, PAIRS))

        def second_product(b):
            butt, top = picked[b]
            last = b * PACK + PACK - 1
            pairs = (slice(0, HALF), slice(HALF, PAIRS))
            z = [ring2.tile([P, HALF, PACK], BF16, name=f"z{hf}", align_bytes=64) for hf in range(2)]

            def smaller(hf):
                nc.vector.tensor_tensor(
                    out=z[hf][:].rearrange("p (c i) t -> p c t i", i=2),
                    in0=butt[:, :, pairs[hf]].rearrange("p t (c i) -> p c t i", i=2),
                    in1=top[:, :, pairs[hf]].rearrange("p t (c i) -> p c t i", i=2),
                    op=ALU.min,
                )

            def multiply(hf):
                z_w = ring2.tile([P, HALF], U32, name=f"z_w{hf}", align_bytes=64)
                z_sc = ring2.tile([P, HALF], U8, name=f"z_sc{hf}", align_bytes=64)
                nc.vector.quantize_mx(out=z_w[:].bitcast(FP8X4), scales=z_sc[:], in_=z[hf][:].rearrange("p m t -> p (m t)"))
                for n in range(N_TILES):
                    nc.tensor.matmul_mx(
                        out=y_ps[(hf, n)][0],
                        lhsT=w4_w[:, b, 2 * n * P : 2 * (n + 1) * P].bitcast(FP4X4),
                        lhsT_scale=w4_sc[:, b, n * P : (n + 1) * P],
                        rhs=z_w[:].bitcast(FP8X4),
                        rhs_scale=z_sc[:],
                        start=(b == 0 and y_ps[(hf, n)][1]),
                        stop=(b == R_PASSES - 1 and y_ps[(hf, n)][2]),
                    )

            pick(last, butt, pos1_sb, pairs[0])
            pick(last, top, pos2_sb, pairs[0])
            pick(last, butt, pos1_sb, pairs[1])
            smaller(0)
            pick(last, top, pos2_sb, pairs[1])
            multiply(0)
            smaller(1)
            multiply(1)

        start_up()
        started = 2
        for i in range(R_TILES):
            b, t = divmod(i, PACK)
            ahead = 1 if i < 2 else 2
            while started <= min(R_TILES - 1, i + ahead):
                product_and_reduce(started)
                started = started + 1
            features_and_pick(i)
            if t < K_PASSES and b + 1 < R_PASSES:
                quantise_w1(b + 1, t)
            if t == PACK - 1:
                second_product(b)

        y = [late.tile([P, PAIRS], F32, name=f"y{n}") for n in range(N_TILES)]
        first = [late.tile([P, CUTS], F32, name=f"first{n}") for n in range(N_TILES)]
        diff = [late.tile([P, CUTS], F32, name=f"diff{n}") for n in range(N_TILES)]
        dist = [late.tile([P, CUTS], F32, name=f"dist{n}") for n in range(N_TILES)]
        res = [late.tile([P, CUTS], F32, name=f"res{n}") for n in range(N_TILES)]
        order = (0, 1, 2, 3)
        for hf in range(2):
            for n in order:
                source = y_ps[(hf, n)][0]
                if hf == 1 and n == 1:
                    nc.vector.tensor_copy(out=y[n][:, hf * HALF : (hf + 1) * HALF], in_=source)
                else:
                    nc.scalar.copy(out=y[n][:, hf * HALF : (hf + 1) * HALF], in_=source)

        def finish(n):
            nc.vector.tensor_tensor(out=res[n][:], in0=dist[n][:], in1=first[n][:], op=ALU.mult)
            nc.sync.dma_start(out=out[n * P : (n + 1) * P, :], in_=res[n][:])

        for pair in (order[:2], order[2:]):
            for n in pair:
                nc.vector.tensor_copy(out=first[n][:], in_=y[n][:].indirect(pos3_sb[:]))
            for n in pair:
                nc.vector.tensor_tensor(out=diff[n][:], in0=y[n][:].indirect(pos4_sb[:]), in1=first[n][:], op=ALU.subtract)
                nc.scalar.activation(out=dist[n][:], in_=diff[n][:], func=ACT.Abs)
        for n in order:
            finish(n)
